import numpy as np
import ml_dtypes


def mxq(x, axis, fmt="e4m3"):
    dtype, down = {"e4m3": (ml_dtypes.float8_e4m3fn, 7), "e5m2": (ml_dtypes.float8_e5m2, 14)}[fmt]
    v = np.moveaxis(np.asarray(x, np.float32).astype(ml_dtypes.bfloat16).astype(np.float64), axis, -1)
    blocks = v.reshape(v.shape[:-1] + (-1, 32))
    amax = np.abs(blocks).max(-1, keepdims=True)
    byte = np.maximum(np.where(amax > 0, np.frexp(amax)[1] - 1 + 127, 0) - down, 1)
    scale = np.exp2(byte - 127.0)
    codes = (blocks / scale).astype(np.float32).astype(dtype).astype(np.float64)
    return np.moveaxis((codes * scale).reshape(v.shape), -1, axis)


WIDE = False


def mx_kscale(k):
    if not WIDE:
        return np.ones(k)
    levels = np.array([10, -10, 5, -5, 0])
    if k % 512:
        return np.exp2(np.random.permutation(np.resize(levels, k // 32))).repeat(32)
    a = np.empty((k // 512, 16))
    for p in range(k // 512):
        a[p, :8] = np.random.permutation(np.resize(levels, 8))
        for g in range(8):
            far = levels[np.abs(levels - a[p, g]) >= 10]
            a[p, g + 8] = far[np.random.randint(len(far))]
    return np.exp2(a.ravel()).repeat(32)


def f64(x):
    return np.asarray(x).astype(np.float64)


def striped(idx):
    return np.tile(idx.reshape(-1, 16).T, (8, 1)).astype(np.uint16)


def unstriped(offs):
    return offs[:16].T.reshape(-1).astype(np.int64)


def pack_weight(w):
    k, n = w.shape
    w = f64(np.asarray(w, np.float32).astype(ml_dtypes.bfloat16)).reshape(k // 32, 32, n)
    amax = np.abs(w).max(1)
    byte = np.clip(np.where(amax > 0, np.frexp(amax)[1] - 1 + 127 - 7, 1), 1, 254)
    scaled = (w * np.exp2(127.0 - byte)[:, None, :]).reshape(k, n).astype(np.float32)
    words = np.ascontiguousarray(scaled.reshape(k // 512, 128, 4, n).transpose(0, 1, 3, 2)).astype(ml_dtypes.float8_e4m3fn).view(np.uint8)
    return words, np.ascontiguousarray(byte.astype(np.uint8).reshape(k // 512, 16, n))


def unpack_weight(words, scales):
    g, p, n, _ = words.shape
    vals = np.ascontiguousarray(words).view(ml_dtypes.float8_e4m3fn).astype(np.float64) * np.repeat(np.exp2(scales.astype(np.float64) - 127.0), 8, axis=1)[..., None]
    return vals.transpose(0, 1, 3, 2).reshape(g * 512, n)


K, T, S, H, Z, W = 512, 1024, 512, 512, 512, 1024
P = 2 ** 7


def setup_inputs():
    n = np.random.standard_normal
    s = mx_kscale(K)[:, None]
    u = mx_kscale(H)
    packed_xT = pack_weight(n((K, T)) * s)
    packed_eT = pack_weight(n((K, W)) * s)
    return {
        "x_words": packed_xT[0],
        "x_scales": packed_xT[1],
        "w1": (n((K, H)) / np.sqrt(K) / s).astype(np.float32),
        "w2": (n((K, H)) / np.sqrt(K) / s).astype(np.float32),
        "e_words": packed_eT[0],
        "e_scales": packed_eT[1],
        "w3": (n((K, H)) / np.sqrt(K) / s).astype(np.float32),
        "unit": (np.random.uniform(0.6, 1.4, (H, 1)) * u[:, None]).astype(np.float32),
        "unit2": (np.random.uniform(0.6, 1.4, (H, 1)) / np.sqrt(H) / u[:, None]).astype(np.float32),
        "vol": (np.tile(np.random.uniform(0.4, 1.5, W), (P, 1))).astype(np.float32),
        "offs": striped(np.random.permutation(T)[:S]),
        "hdg": striped(np.random.permutation(W)[:Z]),
        "sec": striped(np.random.permutation(S)),
        "prx": striped(np.random.permutation(Z)),
    }


def reference(x_words, x_scales, w1, w2, e_words, e_scales, w3, unit, unit2, vol, offs, hdg, sec, prx):
    xq = unpack_weight(x_words, x_scales)[:, unstriped(offs)]
    y = mxq(f64(w1), 0, "e4m3").T @ xq
    yv = mxq(f64(w2), 0, "e4m3").T @ xq
    vs = yv[:, unstriped(sec)]
    load = y + 0.5 * vs
    hid = f64(unit) * load
    e_hdg = unpack_weight(e_words, e_scales)[:, unstriped(hdg)]
    ye = mxq(f64(w3), 0, "e4m3").T @ e_hdg
    hid2 = f64(unit2) * ye
    sc = mxq(hid, 0, "e4m3").T @ mxq(hid2, 0, "e4m3")
    beta_ = sc / (f64(vol)[:1][:, unstriped(hdg)])
    b2 = (beta_) ** 2
    expl = b2.mean(axis=1, keepdims=True)
    return beta_ / (np.sqrt(expl + 0.1) + 0.3) - (0.4 * beta_[:, unstriped(prx)])

@@ -1,0 +1,255 @@
+from contextlib import ExitStack
+
+import concourse.mybir as mybir
+from concourse.masks import make_identity
+
+F32 = mybir.dt.float32
+BF16 = mybir.dt.bfloat16
+I32 = mybir.dt.int32
+U32 = mybir.dt.uint32
+U16 = mybir.dt.uint16
+U8 = mybir.dt.uint8
+FP8X4 = mybir.dt.float8_e4m3fn_x4
+ALU = mybir.AluOpType
+ACT = mybir.ActivationFunctionType
+
+P = 128
+PACK = 4
+N = 512
+STORE = 1024
+HALF = N // 2
+SPARE = 8
+FLOPS = 4 * 2 * N * N * N
+
+
+def tile_picked_yfcovr_beta_p_kernel(
+    tc, x_words, x_scales, w1, w2, e_words, e_scales, w3, unit, unit2, vol, offs, hdg, sec, prx, out
+):
+    nc = tc.nc
+    with ExitStack() as ctx:
+        keep = ctx.enter_context(tc.tile_pool(name="keep", bufs=1))
+        psum = ctx.enter_context(tc.psum_pool(name="psum", bufs=8))
+
+        def sb(name, shape, dtype):
+            return keep.tile(shape, dtype, name=name, align_bytes=64)
+
+        def bank(name):
+            return psum.tile([P, N], F32, name=name, tag="bank")
+
+        def load_list(name, src):
+            t = keep.tile([P, N // 16], U16, name=name)
+            nc.sync.dma_start(t[:], src)
+            return t
+
+        def load_words(name, src):
+            t = sb(name, [P, STORE], U32)
+            nc.sync.dma_start(t[:].bitcast(I32), src[0].rearrange("p n r -> p (n r)").bitcast(I32))
+            return t
+
+        def load_scales(name, src):
+            t = sb(name, [P, STORE], U8)
+            nc.vector.memset(t[:].bitcast(I32), 0)
+            for q in range(4):
+                nc.sync.dma_start(t[32 * q : 32 * q + 4, :].bitcast(I32), src[0, 4 * q : 4 * q + 4, :].bitcast(I32))
+            return t
+
+        def load_weight(name, src):
+            t = sb(name, [P, PACK, N], F32)
+            nc.sync.dma_start(t[:], src.rearrange("(p j) c -> p j c", j=PACK))
+            return t
+
+        def load_rows(name, src):
+            t = sb(name, [P, PACK], F32)
+            nc.sync.dma_start(t[:], src.rearrange("(p t) o -> p (t o)", t=PACK))
+            return t
+
+        def pick(name, window, offsets, dtype):
+            t = sb(name, [P, N], dtype)
+            nc.vector.tensor_copy(t[:], window[:].indirect(offsets[:]))
+            return t
+
+        def round_pair(name, raw, h, on_scalar):
+            t = sb(name, [P, 2 * N], BF16)
+            dst = t[:].rearrange("p (t m j) -> p m j t", t=2, j=PACK)
+            src = raw[:].rearrange("p j (m t) -> p m j t", t=PACK)[:, :, :, 2 * h : 2 * h + 2]
+            if on_scalar:
+                nc.scalar.copy(dst, src)
+            else:
+                nc.vector.tensor_copy(dst, src)
+            return t
+
+        def quantise(name, values):
+            width = values.shape[1] // PACK
+            codes = sb(name + "_codes", [P, width], U32)
+            scales = sb(name + "_scales", [P, width], U8)
+            nc.vector.quantize_mx(codes[:].bitcast(FP8X4), scales[:], values)
+            return codes, scales
+
+        def product(dst, lhs, lhs_cols, rhs, rhs_cols):
+            nc.tensor.matmul_mx(
+                dst,
+                lhsT=lhs[0][:, lhs_cols].bitcast(FP8X4),
+                lhsT_scale=lhs[1][:, lhs_cols],
+                rhs=rhs[0][:, rhs_cols].bitcast(FP8X4),
+                rhs_scale=rhs[1][:, rhs_cols],
+                start=True,
+                stop=True,
+            )
+
+        def block(b):
+            return slice(P * b, P * (b + 1))
+
+        offs_t = load_list("offs_t", offs)
+        x_word_table = load_words("x_word_table", x_words)
+        x_scale_table = load_scales("x_scale_table", x_scales)
+        vol_narrow = sb("vol_narrow", [P, STORE // P], F32)
+        nc.sync.dma_start(vol_narrow[:], vol[0, :].rearrange("(n m) -> n m", n=P))
+        w2_raw = load_weight("w2_raw", w2)
+        hdg_t = load_list("hdg_t", hdg)
+        e_word_table = load_words("e_word_table", e_words)
+        unit_t = load_rows("unit_t", unit)
+        e_scale_table = load_scales("e_scale_table", e_scales)
+        w3_raw = load_weight("w3_raw", w3)
+        sec_t = load_list("sec_t", sec)
+        w1_raw = load_weight("w1_raw", w1)
+        unit2_t = load_rows("unit2_t", unit2)
+        prx_t = load_list("prx_t", prx)
+
+        identity = sb("identity", [P, P], F32)
+        make_identity(nc, identity[:])
+        beta = [sb("beta%d" % b, [P, N + SPARE], F32) for b in range(4)]
+        for b in range(4):
+            nc.gpsimd.memset(beta[b][:, N:], 0.0)
+
+        inv_narrow = sb("inv_narrow", [P, STORE // P], F32)
+        nc.vector.reciprocal(inv_narrow[:], vol_narrow[:])
+        x_picked_words = pick("x_picked_words", x_word_table, offs_t, U32)
+        x_picked = (x_picked_words, pick("x_picked_scales", x_scale_table, offs_t, U8))
+
+        inv_table = sb("inv_table", [P, STORE], F32)
+        for h in range(2):
+            spread = bank("spread%d" % h)
+            for m in range(4):
+                col = 4 * h + m
+                nc.tensor.transpose(spread[:, block(m)], inv_narrow[:, col : col + 1].to_broadcast([P, P]), identity[:])
+            nc.scalar.activation(
+                inv_table[:].rearrange("p (n h m) -> p h n m", h=2, m=4)[:, h],
+                spread[:].rearrange("p (m n) -> p n m", m=4),
+                ACT.Copy,
+                scale=0.4,
+            )
+        inv_vol = sb("inv_vol", [P, N], F32)
+        nc.scalar.activation(inv_vol[:], inv_table[:].indirect(hdg_t[:]), ACT.Copy)
+
+        w2_b = [round_pair("w2_b%d" % h, w2_raw, h, h == 1) for h in range(2)]
+        w2_q = [quantise("w2_q%d" % h, w2_b[h][:]) for h in range(2)]
+        yv = []
+        for t in range(PACK):
+            acc = bank("yv_acc%d" % t)
+            product(acc[:], w2_q[t // 2], block(t % 2), x_picked, slice(0, N))
+            plane = sb("yv%d" % t, [P, N], F32)
+            nc.scalar.activation(plane[:], acc[:], ACT.Copy, scale=unit_t[:, t : t + 1])
+            yv.append(plane)
+
+        e_picked_words = pick("e_picked_words", e_word_table, hdg_t, U32)
+        e_picked = (e_picked_words, pick("e_picked_scales", e_scale_table, hdg_t, U8))
+
+        def sector(h):
+            planes = []
+            for t in range(PACK):
+                g = sb("vs%d_%d" % (h, t), [P, HALF], F32)
+                nc.scalar.activation(g[:], yv[t][:].indirect(sec_t[:, 16 * h : 16 * (h + 1)]), ACT.Copy, scale=0.5)
+                planes.append(g)
+            return planes
+
+        w3_b = [round_pair("w3_b%d" % h, w3_raw, h, h == 1) for h in range(2)]
+        w3_q = [quantise("w3_q%d" % h, w3_b[h][:]) for h in range(2)]
+        w1_b = [round_pair("w1_b%d" % h, w1_raw, h, h == 1) for h in range(2)]
+        vs = [sector(0)]
+        hid2_b = sb("hid2_b", [P, N * PACK], BF16)
+        ye_acc = []
+        for b in range(4):
+            acc = bank("ye_acc%d" % b)
+            for t in range(PACK):
+                product(acc[:, block(t)], w3_q[t // 2], block(t % 2), e_picked, block(b))
+            ye_acc.append(acc)
+        w1_q = [quantise("w1_q%d" % h, w1_b[h][:]) for h in range(2)]
+        y_acc = []
+        for t in range(PACK):
+            acc = bank("y_acc%d" % t)
+            product(acc[:], w1_q[t // 2], block(t % 2), x_picked, slice(0, N))
+            y_acc.append(acc)
+        for b in range(4):
+            nc.vector.tensor_tensor(
+                hid2_b[:, N * b : N * (b + 1)].rearrange("p (n t) -> p n t", t=PACK),
+                ye_acc[b][:].rearrange("p (t n) -> p n t", t=PACK),
+                unit2_t[:].unsqueeze(1).to_broadcast([P, P, PACK]),
+                ALU.mult,
+            )
+        vs.append(sector(1))
+
+        def hid_planes(h):
+            planes = sb("hid_planes%d" % h, [P, PACK, HALF], BF16)
+            for t in range(PACK):
+                nc.vector.scalar_tensor_tensor(
+                    planes[:, t, :], y_acc[t][:, HALF * h : HALF * (h + 1)], unit_t[:, t : t + 1], vs[h][t][:], ALU.mult, ALU.add
+                )
+            return planes
+
+        def weave(h, planes):
+            woven = sb("hid_b%d" % h, [P, PACK * HALF], BF16)
+            nc.vector.tensor_copy(
+                woven[:].rearrange("p (c i t) -> p c t i", i=4, t=PACK), planes[:].rearrange("p t (c i) -> p c t i", i=4)
+            )
+            return woven
+
+        planes0 = hid_planes(0)
+        hid2_q = quantise("hid2_q", hid2_b[:])
+        woven0 = weave(0, planes0)
+
+        def covariances(b, hid_q):
+            acc = bank("sc_acc%d" % b)
+            product(acc[:], hid_q, block(b % 2), hid2_q, slice(0, N))
+            return acc
+
+        def betas(b, acc):
+            nc.vector.tensor_tensor(beta[b][:, :N], acc[:], inv_vol[:], ALU.mult)
+            squares = keep.tile([P, N], BF16, name="squares%d" % b, tag="squares", bufs=2)
+            total = sb("total%d" % b, [P, 1], F32)
+            nc.scalar.activation(squares[:], beta[b][:, :N], ACT.Square, accum_out=total[:])
+            root = sb("root%d" % b, [P, 1], F32)
+            nc.scalar.activation(root[:], total[:], ACT.Sqrt, scale=1.0 / (0.16 * N), bias=0.1)
+            proxy = sb("proxy%d" % b, [P, N], F32)
+            nc.scalar.activation(proxy[:], beta[b][:].indirect(prx_t[:]), ACT.Copy)
+            return proxy, root
+
+        def row_factor(b, root):
+            denom = sb("denom%d" % b, [P, 1], F32)
+            nc.vector.tensor_scalar(denom[:], root[:], 0.4, 0.12, ALU.mult, ALU.add)
+            factor = sb("factor%d" % b, [P, 1], F32)
+            nc.vector.reciprocal(factor[:], denom[:])
+            return factor
+
+        def finish(b, proxy, root):
+            factor = row_factor(b, root)
+            result = sb("result%d" % b, [P, N], F32)
+            nc.vector.scalar_tensor_tensor(result[:], beta[b][:, :N], factor[:], proxy[:], ALU.mult, ALU.subtract)
+            nc.sync.dma_start(out[block(b), :], result[:])
+
+        planes1 = None
+        hid_q0 = quantise("hid_q0", woven0[:])
+        acc0 = covariances(0, hid_q0)
+        acc1 = covariances(1, hid_q0)
+        planes1 = hid_planes(1)
+        parts0 = betas(0, acc0)
+        woven1 = weave(1, planes1)
+        parts1 = betas(1, acc1)
+        hid_q1 = quantise("hid_q1", woven1[:])
+        acc2 = covariances(2, hid_q1)
+        acc3 = covariances(3, hid_q1)
+        finish(0, *parts0)
+        parts2 = betas(2, acc2)
+        parts3 = betas(3, acc3)
+        finish(1, *parts1)
+        finish(2, *parts2)
+        finish(3, *parts3)

@@ -48,9 +48,9 @@ def tile_picked_yfcovr_beta_p_kernel(
 
         def load_scales(name, src):
             t = sb(name, [P, STORE], U8)
-            nc.vector.memset(t[:].bitcast(I32), 0)
             for q in range(4):
-                nc.sync.dma_start(t[32 * q : 32 * q + 4, :].bitcast(I32), src[0, 4 * q : 4 * q + 4, :].bitcast(I32))
+                rows = src[0, 4 * q : 4 * q + 4, :].bitcast(I32)
+                nc.sync.dma_start(t[32 * q : 32 * q + 32, :].bitcast(I32), rows.unsqueeze(0).broadcast_to([8, 4, STORE // 4]))
             return t
 
         def load_weight(name, src):
@@ -60,7 +60,7 @@ def tile_picked_yfcovr_beta_p_kernel(
 
         def load_rows(name, src):
             t = sb(name, [P, PACK], F32)
-            nc.sync.dma_start(t[:], src.rearrange("(p t) o -> p (t o)", t=PACK))
+            nc.gpsimd.dma_start(t[:], src.rearrange("(p t) o -> p (t o)", t=PACK))
             return t
 
         def pick(name, window, offsets, dtype):
@@ -68,14 +68,18 @@ def tile_picked_yfcovr_beta_p_kernel(
             nc.vector.tensor_copy(t[:], window[:].indirect(offsets[:]))
             return t
 
-        def round_pair(name, raw, h, on_scalar):
+        def round_pair(name, raw, h, engine):
             t = sb(name, [P, 2 * N], BF16)
             dst = t[:].rearrange("p (t m j) -> p m j t", t=2, j=PACK)
             src = raw[:].rearrange("p j (m t) -> p m j t", t=PACK)[:, :, :, 2 * h : 2 * h + 2]
-            if on_scalar:
+            if engine == "scalar":
                 nc.scalar.copy(dst, src)
-            else:
+            elif engine == "vector":
                 nc.vector.tensor_copy(dst, src)
+            else:
+                nc.gpsimd.tensor_scalar(
+                    dst.rearrange("p m j t -> p m t j"), src.rearrange("p m j t -> p m t j"), 1.0, 0.0, ALU.mult, ALU.add
+                )
             return t
 
         def quantise(name, values):
@@ -100,31 +104,34 @@ def tile_picked_yfcovr_beta_p_kernel(
             return slice(P * b, P * (b + 1))
 
         offs_t = load_list("offs_t", offs)
-        x_word_table = load_words("x_word_table", x_words)
-        x_scale_table = load_scales("x_scale_table", x_scales)
         vol_narrow = sb("vol_narrow", [P, STORE // P], F32)
         nc.sync.dma_start(vol_narrow[:], vol[0, :].rearrange("(n m) -> n m", n=P))
+        x_scale_table = load_scales("x_scale_table", x_scales)
+        x_word_table = load_words("x_word_table", x_words)
         w2_raw = load_weight("w2_raw", w2)
         hdg_t = load_list("hdg_t", hdg)
         e_word_table = load_words("e_word_table", e_words)
-        unit_t = load_rows("unit_t", unit)
         e_scale_table = load_scales("e_scale_table", e_scales)
         w3_raw = load_weight("w3_raw", w3)
         sec_t = load_list("sec_t", sec)
         w1_raw = load_weight("w1_raw", w1)
-        unit2_t = load_rows("unit2_t", unit2)
         prx_t = load_list("prx_t", prx)
-
         identity = sb("identity", [P, P], F32)
         make_identity(nc, identity[:])
+        unit_t = load_rows("unit_t", unit)
+        unit2_t = load_rows("unit2_t", unit2)
+        warm_in = sb("warm_in", [P, 1], F32)
+        nc.vector.memset(warm_in[:], 1.0)
+        warm_out = sb("warm_out", [P, 1], F32)
+        nc.scalar.activation(warm_out[:], warm_in[:], ACT.Sqrt)
         beta = [sb("beta%d" % b, [P, N + SPARE], F32) for b in range(4)]
         for b in range(4):
             nc.gpsimd.memset(beta[b][:, N:], 0.0)
 
         inv_narrow = sb("inv_narrow", [P, STORE // P], F32)
         nc.vector.reciprocal(inv_narrow[:], vol_narrow[:])
-        x_picked_words = pick("x_picked_words", x_word_table, offs_t, U32)
-        x_picked = (x_picked_words, pick("x_picked_scales", x_scale_table, offs_t, U8))
+        x_picked_scales = pick("x_picked_scales", x_scale_table, offs_t, U8)
+        x_picked = (pick("x_picked_words", x_word_table, offs_t, U32), x_picked_scales)
 
         inv_table = sb("inv_table", [P, STORE], F32)
         for h in range(2):
@@ -138,11 +145,11 @@ def tile_picked_yfcovr_beta_p_kernel(
                 ACT.Copy,
                 scale=0.4,
             )
+
+        w2_b = [round_pair("w2_b%d" % h, w2_raw, h, ["vector","scalar"][h]) for h in range(2)]
+        w2_q = [quantise("w2_q%d" % h, w2_b[h][:]) for h in range(2)]
         inv_vol = sb("inv_vol", [P, N], F32)
         nc.scalar.activation(inv_vol[:], inv_table[:].indirect(hdg_t[:]), ACT.Copy)
-
-        w2_b = [round_pair("w2_b%d" % h, w2_raw, h, h == 1) for h in range(2)]
-        w2_q = [quantise("w2_q%d" % h, w2_b[h][:]) for h in range(2)]
         yv = []
         for t in range(PACK):
             acc = bank("yv_acc%d" % t)
@@ -162,9 +169,8 @@ def tile_picked_yfcovr_beta_p_kernel(
                 planes.append(g)
             return planes
 
-        w3_b = [round_pair("w3_b%d" % h, w3_raw, h, h == 1) for h in range(2)]
+        w3_b = [round_pair("w3_b%d" % h, w3_raw, h, ["vector","gpsimd"][h]) for h in range(2)]
         w3_q = [quantise("w3_q%d" % h, w3_b[h][:]) for h in range(2)]
-        w1_b = [round_pair("w1_b%d" % h, w1_raw, h, h == 1) for h in range(2)]
         vs = [sector(0)]
         hid2_b = sb("hid2_b", [P, N * PACK], BF16)
         ye_acc = []
@@ -173,12 +179,6 @@ def tile_picked_yfcovr_beta_p_kernel(
             for t in range(PACK):
                 product(acc[:, block(t)], w3_q[t // 2], block(t % 2), e_picked, block(b))
             ye_acc.append(acc)
-        w1_q = [quantise("w1_q%d" % h, w1_b[h][:]) for h in range(2)]
-        y_acc = []
-        for t in range(PACK):
-            acc = bank("y_acc%d" % t)
-            product(acc[:], w1_q[t // 2], block(t % 2), x_picked, slice(0, N))
-            y_acc.append(acc)
         for b in range(4):
             nc.vector.tensor_tensor(
                 hid2_b[:, N * b : N * (b + 1)].rearrange("p (n t) -> p n t", t=PACK),
@@ -186,6 +186,14 @@ def tile_picked_yfcovr_beta_p_kernel(
                 unit2_t[:].unsqueeze(1).to_broadcast([P, P, PACK]),
                 ALU.mult,
             )
+        hid2_q = quantise("hid2_q", hid2_b[:])
+        w1_b = [round_pair("w1_b%d" % h, w1_raw, h, ["gpsimd","gpsimd"][h]) for h in range(2)]
+        w1_q = [quantise("w1_q%d" % h, w1_b[h][:]) for h in range(2)]
+        y_acc = []
+        for t in range(PACK):
+            acc = bank("y_acc%d" % t)
+            product(acc[:], w1_q[t // 2], block(t % 2), x_picked, slice(0, N))
+            y_acc.append(acc)
         vs.append(sector(1))
 
         def hid_planes(h):
@@ -196,16 +204,15 @@ def tile_picked_yfcovr_beta_p_kernel(
                 )
             return planes
 
-        def weave(h, planes):
+        def weave(h, planes, on_scalar):
             woven = sb("hid_b%d" % h, [P, PACK * HALF], BF16)
-            nc.vector.tensor_copy(
-                woven[:].rearrange("p (c i t) -> p c t i", i=4, t=PACK), planes[:].rearrange("p t (c i) -> p c t i", i=4)
-            )
+            dst = woven[:].rearrange("p (c i t) -> p c t i", i=4, t=PACK)
+            src = planes[:].rearrange("p t (c i) -> p c t i", i=4)
+            if on_scalar:
+                nc.scalar.copy(dst, src)
+            else:
+                nc.vector.tensor_copy(dst, src)
             return woven
-
-        planes0 = hid_planes(0)
-        hid2_q = quantise("hid2_q", hid2_b[:])
-        woven0 = weave(0, planes0)
 
         def covariances(b, hid_q):
             acc = bank("sc_acc%d" % b)
@@ -219,37 +226,45 @@ def tile_picked_yfcovr_beta_p_kernel(
             nc.scalar.activation(squares[:], beta[b][:, :N], ACT.Square, accum_out=total[:])
             root = sb("root%d" % b, [P, 1], F32)
             nc.scalar.activation(root[:], total[:], ACT.Sqrt, scale=1.0 / (0.16 * N), bias=0.1)
-            proxy = sb("proxy%d" % b, [P, N], F32)
-            nc.scalar.activation(proxy[:], beta[b][:].indirect(prx_t[:]), ACT.Copy)
-            return proxy, root
-
-        def row_factor(b, root):
             denom = sb("denom%d" % b, [P, 1], F32)
             nc.vector.tensor_scalar(denom[:], root[:], 0.4, 0.12, ALU.mult, ALU.add)
             factor = sb("factor%d" % b, [P, 1], F32)
             nc.vector.reciprocal(factor[:], denom[:])
             return factor
 
-        def finish(b, proxy, root):
-            factor = row_factor(b, root)
-            result = sb("result%d" % b, [P, N], F32)
-            nc.vector.scalar_tensor_tensor(result[:], beta[b][:, :N], factor[:], proxy[:], ALU.mult, ALU.subtract)
-            nc.sync.dma_start(out[block(b), :], result[:])
+        def proxies(b, lo, hi, on_scalar):
+            proxy = sb("proxy%d_%d" % (b, lo), [P, hi - lo], F32)
+            if on_scalar:
+                nc.scalar.activation(proxy[:], beta[b][:].indirect(prx_t[:, lo // 16 : hi // 16]), ACT.Copy)
+            else:
+                for h in range(2):
+                    nc.vector.tensor_copy(proxy[:, HALF * h : HALF * (h + 1)], beta[b][:].indirect(prx_t[:, 16 * h : 16 * (h + 1)]))
+            return proxy
 
-        planes1 = None
+        def finish(b, lo, hi, proxy, factor):
+            result = sb("result%d_%d" % (b, lo), [P, hi - lo], F32)
+            nc.vector.scalar_tensor_tensor(result[:], beta[b][:, lo:hi], factor[:], proxy[:], ALU.mult, ALU.subtract)
+            nc.sync.dma_start(out[block(b), lo:hi], result[:])
+
+        planes0 = hid_planes(0)
+        woven0 = weave(0, planes0, True)
         hid_q0 = quantise("hid_q0", woven0[:])
         acc0 = covariances(0, hid_q0)
         acc1 = covariances(1, hid_q0)
+        factor0 = betas(0, acc0)
+        factor1 = betas(1, acc1)
+        proxy0 = proxies(0, 0, N, True)
+        proxy1 = proxies(1, 0, N, True)
         planes1 = hid_planes(1)
-        parts0 = betas(0, acc0)
-        woven1 = weave(1, planes1)
-        parts1 = betas(1, acc1)
+        woven1 = weave(1, planes1, False)
         hid_q1 = quantise("hid_q1", woven1[:])
         acc2 = covariances(2, hid_q1)
         acc3 = covariances(3, hid_q1)
-        finish(0, *parts0)
-        parts2 = betas(2, acc2)
-        parts3 = betas(3, acc3)
-        finish(1, *parts1)
-        finish(2, *parts2)
-        finish(3, *parts3)
+        factor2 = betas(2, acc2)
+        factor3 = betas(3, acc3)
+        finish(0, 0, N, proxy0, factor0)
+        proxy2 = proxies(2, 0, N, False)
+        finish(1, 0, N, proxy1, factor1)
+        finish(2, 0, N, proxy2, factor2)
+        for lo in (0, HALF):
+            finish(3, lo, lo + HALF, proxies(3, lo, lo + HALF, True), factor3)

@@ -54,7 +54,7 @@ def tile_picked_yfcovr_beta_p_kernel(
             return t
 
         def load_weight(name, src):
-            t = sb(name, [P, PACK, N], F32)
+            t = keep.tile([P, PACK, N], F32, name=name, tag=name, align_bytes=64)
             nc.sync.dma_start(t[:], src.rearrange("(p j) c -> p j c", j=PACK))
             return t
 
@@ -108,10 +108,10 @@ def tile_picked_yfcovr_beta_p_kernel(
         nc.sync.dma_start(vol_narrow[:], vol[0, :].rearrange("(n m) -> n m", n=P))
         x_scale_table = load_scales("x_scale_table", x_scales)
         x_word_table = load_words("x_word_table", x_words)
-        w2_raw = load_weight("w2_raw", w2)
         hdg_t = load_list("hdg_t", hdg)
         e_word_table = load_words("e_word_table", e_words)
         e_scale_table = load_scales("e_scale_table", e_scales)
+        w2_raw = load_weight("w2_raw", w2)
         w3_raw = load_weight("w3_raw", w3)
         sec_t = load_list("sec_t", sec)
         w1_raw = load_weight("w1_raw", w1)
@@ -146,10 +146,12 @@ def tile_picked_yfcovr_beta_p_kernel(
                 scale=0.4,
             )
 
-        w2_b = [round_pair("w2_b%d" % h, w2_raw, h, ["vector","scalar"][h]) for h in range(2)]
-        w2_q = [quantise("w2_q%d" % h, w2_b[h][:]) for h in range(2)]
         inv_vol = sb("inv_vol", [P, N], F32)
         nc.scalar.activation(inv_vol[:], inv_table[:].indirect(hdg_t[:]), ACT.Copy)
+        e_picked_words = pick("e_picked_words", e_word_table, hdg_t, U32)
+        e_picked = (e_picked_words, pick("e_picked_scales", e_scale_table, hdg_t, U8))
+        w2_b = [round_pair("w2_b%d" % h, w2_raw, h, ["vector","scalar"][h]) for h in range(2)]
+        w2_q = [quantise("w2_q%d" % h, w2_b[h][:]) for h in range(2)]
         yv = []
         for t in range(PACK):
             acc = bank("yv_acc%d" % t)
@@ -158,19 +160,19 @@ def tile_picked_yfcovr_beta_p_kernel(
             nc.scalar.activation(plane[:], acc[:], ACT.Copy, scale=unit_t[:, t : t + 1])
             yv.append(plane)
 
-        e_picked_words = pick("e_picked_words", e_word_table, hdg_t, U32)
-        e_picked = (e_picked_words, pick("e_picked_scales", e_scale_table, hdg_t, U8))
 
         def sector(h):
             planes = []
             for t in range(PACK):
-                g = sb("vs%d_%d" % (h, t), [P, HALF], F32)
-                nc.scalar.activation(g[:], yv[t][:].indirect(sec_t[:, 16 * h : 16 * (h + 1)]), ACT.Copy, scale=0.5)
+                g = sector_values[:, PACK * h + t, :]
+                nc.scalar.activation(g, yv[t][:].indirect(sec_t[:, 16 * h : 16 * (h + 1)]), ACT.Copy, scale=0.5)
                 planes.append(g)
             return planes
 
-        w3_b = [round_pair("w3_b%d" % h, w3_raw, h, ["vector","gpsimd"][h]) for h in range(2)]
+        w3_b = [round_pair("w3_b%d" % h, w3_raw, h, ["vector","vector"][h]) for h in range(2)]
         w3_q = [quantise("w3_q%d" % h, w3_b[h][:]) for h in range(2)]
+        w1_b = [round_pair("w1_b%d" % h, w1_raw, h, ["scalar","scalar"][h]) for h in range(2)]
+        sector_values = keep.tile([P, 2 * PACK, HALF], F32, name="sector_values", tag="w1_raw", align_bytes=64)
         vs = [sector(0)]
         hid2_b = sb("hid2_b", [P, N * PACK], BF16)
         ye_acc = []
@@ -186,9 +188,8 @@ def tile_picked_yfcovr_beta_p_kernel(
                 unit2_t[:].unsqueeze(1).to_broadcast([P, P, PACK]),
                 ALU.mult,
             )
-        hid2_q = quantise("hid2_q", hid2_b[:])
-        w1_b = [round_pair("w1_b%d" % h, w1_raw, h, ["gpsimd","gpsimd"][h]) for h in range(2)]
         w1_q = [quantise("w1_q%d" % h, w1_b[h][:]) for h in range(2)]
+        hid2_q = quantise("hid2_q", hid2_b[:])
         y_acc = []
         for t in range(PACK):
             acc = bank("y_acc%d" % t)
@@ -197,15 +198,15 @@ def tile_picked_yfcovr_beta_p_kernel(
         vs.append(sector(1))
 
         def hid_planes(h):
-            planes = sb("hid_planes%d" % h, [P, PACK, HALF], BF16)
+            planes = keep.tile([P, PACK, HALF], BF16, name="hid_planes%d" % h, tag="hid_planes", align_bytes=64)
             for t in range(PACK):
                 nc.vector.scalar_tensor_tensor(
-                    planes[:, t, :], y_acc[t][:, HALF * h : HALF * (h + 1)], unit_t[:, t : t + 1], vs[h][t][:], ALU.mult, ALU.add
+                    planes[:, t, :], y_acc[t][:, HALF * h : HALF * (h + 1)], unit_t[:, t : t + 1], vs[h][t], ALU.mult, ALU.add
                 )
             return planes
 
         def weave(h, planes, on_scalar):
-            woven = sb("hid_b%d" % h, [P, PACK * HALF], BF16)
+            woven = keep.tile([P, PACK * HALF], BF16, name="hid_b%d" % h, tag="hid_b%d" % h, align_bytes=64)
             dst = woven[:].rearrange("p (c i t) -> p c t i", i=4, t=PACK)
             src = planes[:].rearrange("p t (c i) -> p c t i", i=4)
             if on_scalar:
@@ -219,52 +220,66 @@ def tile_picked_yfcovr_beta_p_kernel(
             product(acc[:], hid_q, block(b % 2), hid2_q, slice(0, N))
             return acc
 
-        def betas(b, acc):
+        def betas(b, acc, total):
             nc.vector.tensor_tensor(beta[b][:, :N], acc[:], inv_vol[:], ALU.mult)
             squares = keep.tile([P, N], BF16, name="squares%d" % b, tag="squares", bufs=2)
-            total = sb("total%d" % b, [P, 1], F32)
-            nc.scalar.activation(squares[:], beta[b][:, :N], ACT.Square, accum_out=total[:])
-            root = sb("root%d" % b, [P, 1], F32)
-            nc.scalar.activation(root[:], total[:], ACT.Sqrt, scale=1.0 / (0.16 * N), bias=0.1)
-            denom = sb("denom%d" % b, [P, 1], F32)
+            nc.scalar.activation(squares[:], beta[b][:, :N], ACT.Square, accum_out=total)
+
+        def roots(h, totals):
+            root = sb("root%d" % h, [P, 2], F32)
+            nc.scalar.activation(root[:], totals[:], ACT.Sqrt, scale=1.0 / (0.16 * N), bias=0.1)
+            return root
+
+        def factors(h, root, denom):
             nc.vector.tensor_scalar(denom[:], root[:], 0.4, 0.12, ALU.mult, ALU.add)
-            factor = sb("factor%d" % b, [P, 1], F32)
+            factor = sb("factor%d" % h, [P, 2], F32)
             nc.vector.reciprocal(factor[:], denom[:])
             return factor
 
-        def proxies(b, lo, hi, on_scalar):
-            proxy = sb("proxy%d_%d" % (b, lo), [P, hi - lo], F32)
-            if on_scalar:
-                nc.scalar.activation(proxy[:], beta[b][:].indirect(prx_t[:, lo // 16 : hi // 16]), ACT.Copy)
-            else:
-                for h in range(2):
-                    nc.vector.tensor_copy(proxy[:, HALF * h : HALF * (h + 1)], beta[b][:].indirect(prx_t[:, 16 * h : 16 * (h + 1)]))
-            return proxy
+        def looked_up(b, lo, hi):
+            return beta[b][:].indirect(prx_t[:, lo // 16 : hi // 16])
 
-        def finish(b, lo, hi, proxy, factor):
+        def finish(b, lo, hi, factor, proxy):
             result = sb("result%d_%d" % (b, lo), [P, hi - lo], F32)
-            nc.vector.scalar_tensor_tensor(result[:], beta[b][:, lo:hi], factor[:], proxy[:], ALU.mult, ALU.subtract)
+            nc.vector.scalar_tensor_tensor(
+                result[:], beta[b][:, lo:hi], factor[:, b % 2 : b % 2 + 1], proxy, ALU.mult, ALU.subtract
+            )
             nc.sync.dma_start(out[block(b), lo:hi], result[:])
 
+        def shared(name, tag, shape, dtype):
+            return keep.tile(shape, dtype, name=name, tag=tag, align_bytes=64)
+
         planes0 = hid_planes(0)
-        woven0 = weave(0, planes0, True)
+        woven0 = weave(0, planes0, False)
         hid_q0 = quantise("hid_q0", woven0[:])
         acc0 = covariances(0, hid_q0)
         acc1 = covariances(1, hid_q0)
-        factor0 = betas(0, acc0)
-        factor1 = betas(1, acc1)
-        proxy0 = proxies(0, 0, N, True)
-        proxy1 = proxies(1, 0, N, True)
+        totals0 = shared("totals0", "proxies0", [P, 2], F32)
+        betas(0, acc0, totals0[:, 0:1])
+        betas(1, acc1, totals0[:, 1:2])
+        root0 = roots(0, totals0)
+        proxies0 = shared("proxies0", "proxies0", [P, 2, N], F32)
+        for b in range(2):
+            nc.scalar.activation(proxies0[:, b, :], looked_up(b, 0, N), ACT.Copy)
         planes1 = hid_planes(1)
         woven1 = weave(1, planes1, False)
         hid_q1 = quantise("hid_q1", woven1[:])
+        factor0 = factors(0, root0, shared("denom0", "hid_b1", [P, 2], F32))
         acc2 = covariances(2, hid_q1)
         acc3 = covariances(3, hid_q1)
-        factor2 = betas(2, acc2)
-        factor3 = betas(3, acc3)
-        finish(0, 0, N, proxy0, factor0)
-        proxy2 = proxies(2, 0, N, False)
-        finish(1, 0, N, proxy1, factor1)
-        finish(2, 0, N, proxy2, factor2)
-        for lo in (0, HALF):
-            finish(3, lo, lo + HALF, proxies(3, lo, lo + HALF, True), factor3)
+        totals1 = shared("totals1", "proxies1", [P, 2], F32)
+        betas(2, acc2, totals1[:, 0:1])
+        betas(3, acc3, totals1[:, 1:2])
+        root1 = roots(1, totals1)
+        finish(0, 0, N, factor0, proxies0[:, 0, :])
+        proxy_first = sb("proxy_first", [P, HALF], F32)
+        nc.vector.tensor_copy(proxy_first[:], looked_up(2, 0, HALF))
+        proxies1 = shared("proxies1", "proxies1", [P, 3, HALF], F32)
+        pieces = [(2, HALF), (3, 0), (3, HALF)]
+        for i, (b, lo) in enumerate(pieces):
+            nc.scalar.activation(proxies1[:, i, :], looked_up(b, lo, lo + HALF), ACT.Copy)
+        finish(1, 0, N, factor0, proxies0[:, 1, :])
+        factor1 = factors(1, root1, sb("denom1", [P, 2], F32))
+        finish(2, 0, HALF, factor1, proxy_first[:])
+        for i, (b, lo) in enumerate(pieces):
+            finish(b, lo, lo + HALF, factor1, proxies1[:, i, :])

@@ -48,9 +48,9 @@ def tile_picked_yfcovr_beta_p_kernel(
 
         def load_scales(name, src):
             t = sb(name, [P, STORE], U8)
+            nc.gpsimd.memset(t[:].bitcast(I32), 0)
             for q in range(4):
-                rows = src[0, 4 * q : 4 * q + 4, :].bitcast(I32)
-                nc.sync.dma_start(t[32 * q : 32 * q + 32, :].bitcast(I32), rows.unsqueeze(0).broadcast_to([8, 4, STORE // 4]))
+                nc.sync.dma_start(t[32 * q : 32 * q + 4, :].bitcast(I32), src[0, 4 * q : 4 * q + 4, :].bitcast(I32))
             return t
 
         def load_weight(name, src):
@@ -171,7 +171,7 @@ def tile_picked_yfcovr_beta_p_kernel(
 
         w3_b = [round_pair("w3_b%d" % h, w3_raw, h, ["vector","vector"][h]) for h in range(2)]
         w3_q = [quantise("w3_q%d" % h, w3_b[h][:]) for h in range(2)]
-        w1_b = [round_pair("w1_b%d" % h, w1_raw, h, ["scalar","scalar"][h]) for h in range(2)]
+        w1_b = [round_pair("w1_b%d" % h, w1_raw, h, ["scalar","gpsimd"][h]) for h in range(2)]
         sector_values = keep.tile([P, 2 * PACK, HALF], F32, name="sector_values", tag="w1_raw", align_bytes=64)
         vs = [sector(0)]
         hid2_b = sb("hid2_b", [P, N * PACK], BF16)
@@ -183,9 +183,9 @@ def tile_picked_yfcovr_beta_p_kernel(
             ye_acc.append(acc)
         for b in range(4):
             nc.vector.tensor_tensor(
-                hid2_b[:, N * b : N * (b + 1)].rearrange("p (n t) -> p n t", t=PACK),
-                ye_acc[b][:].rearrange("p (t n) -> p n t", t=PACK),
-                unit2_t[:].unsqueeze(1).to_broadcast([P, P, PACK]),
+                hid2_b[:, N * b : N * (b + 1)].rearrange("p (c i t) -> p c t i", i=2, t=PACK),
+                ye_acc[b][:].rearrange("p (t c i) -> p c t i", i=2, t=PACK),
+                unit2_t[:].unsqueeze(1).unsqueeze(3).to_broadcast([P, P // 2, PACK, 2]),
                 ALU.mult,
             )
         w1_q = [quantise("w1_q%d" % h, w1_b[h][:]) for h in range(2)]

@@ -18,7 +18,10 @@ PACK = 4
 N = 512
 STORE = 1024
 HALF = N // 2
+ENTRIES = 16
 SPARE = 8
+CUT = 384
+BANKS = 8
 FLOPS = 4 * 2 * N * N * N
 
 
@@ -28,50 +31,56 @@ def tile_picked_yfcovr_beta_p_kernel(
     nc = tc.nc
     with ExitStack() as ctx:
         keep = ctx.enter_context(tc.tile_pool(name="keep", bufs=1))
-        psum = ctx.enter_context(tc.psum_pool(name="psum", bufs=8))
+        psum = ctx.enter_context(tc.psum_pool(name="psum", bufs=BANKS))
 
-        def sb(name, shape, dtype):
-            return keep.tile(shape, dtype, name=name, align_bytes=64)
+        def sbuf(name, shape, dtype, after=None):
+            return keep.tile(shape, dtype, name=name, tag=after or name, align_bytes=64)
 
         def bank(name):
             return psum.tile([P, N], F32, name=name, tag="bank")
 
+        def block(b):
+            return slice(P * b, P * (b + 1))
+
+        def entries(list_tile, lo, hi):
+            return list_tile[:, lo // ENTRIES : hi // ENTRIES]
+
         def load_list(name, src):
-            t = keep.tile([P, N // 16], U16, name=name)
-            nc.sync.dma_start(t[:], src)
-            return t
+            tile = keep.tile([P, N // ENTRIES], U16, name=name)
+            nc.sync.dma_start(tile[:], src)
+            return tile
 
         def load_words(name, src):
-            t = sb(name, [P, STORE], U32)
-            nc.sync.dma_start(t[:].bitcast(I32), src[0].rearrange("p n r -> p (n r)").bitcast(I32))
-            return t
+            tile = sbuf(name, [P, STORE], U32)
+            nc.sync.dma_start(tile[:].bitcast(I32), src[0].rearrange("p n r -> p (n r)").bitcast(I32))
+            return tile
 
         def load_scales(name, src):
-            t = sb(name, [P, STORE], U8)
-            nc.gpsimd.memset(t[:].bitcast(I32), 0)
+            tile = sbuf(name, [P, STORE], U8)
+            nc.gpsimd.memset(tile[:].bitcast(I32), 0)
             for q in range(4):
-                nc.sync.dma_start(t[32 * q : 32 * q + 4, :].bitcast(I32), src[0, 4 * q : 4 * q + 4, :].bitcast(I32))
-            return t
+                nc.sync.dma_start(tile[32 * q : 32 * q + 4, :].bitcast(I32), src[0, 4 * q : 4 * q + 4, :].bitcast(I32))
+            return tile
 
         def load_weight(name, src):
-            t = keep.tile([P, PACK, N], F32, name=name, tag=name, align_bytes=64)
-            nc.sync.dma_start(t[:], src.rearrange("(p j) c -> p j c", j=PACK))
-            return t
+            tile = sbuf(name, [P, PACK, N], F32)
+            nc.sync.dma_start(tile[:], src.rearrange("(p j) c -> p j c", j=PACK))
+            return tile
 
-        def load_rows(name, src):
-            t = sb(name, [P, PACK], F32)
-            nc.gpsimd.dma_start(t[:], src.rearrange("(p t) o -> p (t o)", t=PACK))
-            return t
+        def load_row_factors(name, src):
+            tile = sbuf(name, [P, PACK], F32)
+            nc.gpsimd.dma_start(tile[:], src.rearrange("(p t) o -> p (t o)", t=PACK))
+            return tile
 
-        def pick(name, window, offsets, dtype):
-            t = sb(name, [P, N], dtype)
-            nc.vector.tensor_copy(t[:], window[:].indirect(offsets[:]))
-            return t
+        def pick(name, table, list_tile, dtype):
+            tile = sbuf(name, [P, N], dtype)
+            nc.vector.tensor_copy(tile[:], table[:].indirect(list_tile[:]))
+            return tile
 
-        def round_pair(name, raw, h, engine):
-            t = sb(name, [P, 2 * N], BF16)
-            dst = t[:].rearrange("p (t m j) -> p m j t", t=2, j=PACK)
-            src = raw[:].rearrange("p j (m t) -> p m j t", t=PACK)[:, :, :, 2 * h : 2 * h + 2]
+        def round_pair(name, raw, pair, engine):
+            tile = sbuf(name, [P, 2 * N], BF16)
+            dst = tile[:].rearrange("p (t m j) -> p m j t", t=2, j=PACK)
+            src = raw[:].rearrange("p j (m t) -> p m j t", t=PACK)[:, :, :, 2 * pair : 2 * pair + 2]
             if engine == "scalar":
                 nc.scalar.copy(dst, src)
             elif engine == "vector":
@@ -80,13 +89,13 @@ def tile_picked_yfcovr_beta_p_kernel(
                 nc.gpsimd.tensor_scalar(
                     dst.rearrange("p m j t -> p m t j"), src.rearrange("p m j t -> p m t j"), 1.0, 0.0, ALU.mult, ALU.add
                 )
-            return t
+            return tile
 
         def quantise(name, values):
             width = values.shape[1] // PACK
-            codes = sb(name + "_codes", [P, width], U32)
-            scales = sb(name + "_scales", [P, width], U8)
-            nc.vector.quantize_mx(codes[:].bitcast(FP8X4), scales[:], values)
+            codes = sbuf(name + "_codes", [P, width], U32)
+            scales = sbuf(name + "_scales", [P, width], U8)
+            nc.vector.quantize_mx(codes[:].bitcast(FP8X4), scales[:], values[:])
             return codes, scales
 
         def product(dst, lhs, lhs_cols, rhs, rhs_cols):
@@ -100,186 +109,190 @@ def tile_picked_yfcovr_beta_p_kernel(
                 stop=True,
             )
 
-        def block(b):
-            return slice(P * b, P * (b + 1))
+        every = slice(0, N)
 
-        offs_t = load_list("offs_t", offs)
-        vol_narrow = sb("vol_narrow", [P, STORE // P], F32)
+        offs_list = load_list("offs_list", offs)
+        vol_narrow = sbuf("vol_narrow", [P, STORE // P], F32)
         nc.sync.dma_start(vol_narrow[:], vol[0, :].rearrange("(n m) -> n m", n=P))
         x_scale_table = load_scales("x_scale_table", x_scales)
         x_word_table = load_words("x_word_table", x_words)
-        hdg_t = load_list("hdg_t", hdg)
         e_word_table = load_words("e_word_table", e_words)
+        hdg_list = load_list("hdg_list", hdg)
         e_scale_table = load_scales("e_scale_table", e_scales)
         w2_raw = load_weight("w2_raw", w2)
         w3_raw = load_weight("w3_raw", w3)
-        sec_t = load_list("sec_t", sec)
+        sec_list = load_list("sec_list", sec)
         w1_raw = load_weight("w1_raw", w1)
-        prx_t = load_list("prx_t", prx)
-        identity = sb("identity", [P, P], F32)
+        prx_list = load_list("prx_list", prx)
+        identity = sbuf("identity", [P, P], F32)
         make_identity(nc, identity[:])
-        unit_t = load_rows("unit_t", unit)
-        unit2_t = load_rows("unit2_t", unit2)
-        warm_in = sb("warm_in", [P, 1], F32)
+        unit_rows = load_row_factors("unit_rows", unit)
+        unit2_rows = load_row_factors("unit2_rows", unit2)
+
+        warm_in = sbuf("warm_in", [P, 1], F32)
         nc.vector.memset(warm_in[:], 1.0)
-        warm_out = sb("warm_out", [P, 1], F32)
+        warm_out = sbuf("warm_out", [P, 1], F32)
         nc.scalar.activation(warm_out[:], warm_in[:], ACT.Sqrt)
-        beta = [sb("beta%d" % b, [P, N + SPARE], F32) for b in range(4)]
-        for b in range(4):
-            nc.gpsimd.memset(beta[b][:, N:], 0.0)
 
-        inv_narrow = sb("inv_narrow", [P, STORE // P], F32)
+        scaled_beta = [sbuf("scaled_beta%d" % b, [P, N + SPARE], F32) for b in range(N // P)]
+        for b in range(N // P):
+            nc.gpsimd.memset(scaled_beta[b][:, N:], 0.0)
+
+        inv_narrow = sbuf("inv_narrow", [P, STORE // P], F32)
         nc.vector.reciprocal(inv_narrow[:], vol_narrow[:])
-        x_picked_scales = pick("x_picked_scales", x_scale_table, offs_t, U8)
-        x_picked = (pick("x_picked_words", x_word_table, offs_t, U32), x_picked_scales)
-
-        inv_table = sb("inv_table", [P, STORE], F32)
+        x_picked_scales = pick("x_picked_scales", x_scale_table, offs_list, U8)
+        x_picked = (pick("x_picked_words", x_word_table, offs_list, U32), x_picked_scales)
+        inv_table = sbuf("inv_table", [P, STORE], F32)
         for h in range(2):
             spread = bank("spread%d" % h)
             for m in range(4):
-                col = 4 * h + m
-                nc.tensor.transpose(spread[:, block(m)], inv_narrow[:, col : col + 1].to_broadcast([P, P]), identity[:])
+                column = inv_narrow[:, 4 * h + m : 4 * h + m + 1]
+                nc.tensor.transpose(spread[:, block(m)], column.to_broadcast([P, P]), identity[:])
             nc.scalar.activation(
                 inv_table[:].rearrange("p (n h m) -> p h n m", h=2, m=4)[:, h],
                 spread[:].rearrange("p (m n) -> p n m", m=4),
                 ACT.Copy,
                 scale=0.4,
             )
+        inv_vol = sbuf("inv_vol", [P, N], F32)
+        nc.scalar.activation(inv_vol[:], inv_table[:].indirect(hdg_list[:]), ACT.Copy)
 
-        inv_vol = sb("inv_vol", [P, N], F32)
-        nc.scalar.activation(inv_vol[:], inv_table[:].indirect(hdg_t[:]), ACT.Copy)
-        e_picked_words = pick("e_picked_words", e_word_table, hdg_t, U32)
-        e_picked = (e_picked_words, pick("e_picked_scales", e_scale_table, hdg_t, U8))
-        w2_b = [round_pair("w2_b%d" % h, w2_raw, h, ["vector","scalar"][h]) for h in range(2)]
-        w2_q = [quantise("w2_q%d" % h, w2_b[h][:]) for h in range(2)]
-        yv = []
+        e_picked_words = pick("e_picked_words", e_word_table, hdg_list, U32)
+        e_picked = (e_picked_words, pick("e_picked_scales", e_scale_table, hdg_list, U8))
+
+        w2_rounded = [round_pair("w2_rounded%d" % pair, w2_raw, pair, ("vector", "scalar")[pair]) for pair in range(2)]
+        w2_mx = [quantise("w2_mx%d" % pair, w2_rounded[pair]) for pair in range(2)]
+        yv_planes = []
         for t in range(PACK):
             acc = bank("yv_acc%d" % t)
-            product(acc[:], w2_q[t // 2], block(t % 2), x_picked, slice(0, N))
-            plane = sb("yv%d" % t, [P, N], F32)
-            nc.scalar.activation(plane[:], acc[:], ACT.Copy, scale=unit_t[:, t : t + 1])
-            yv.append(plane)
+            product(acc[:], w2_mx[t // 2], block(t % 2), x_picked, every)
+            plane = sbuf("yv_plane%d" % t, [P, N], F32)
+            nc.scalar.activation(plane[:], acc[:], ACT.Copy, scale=unit_rows[:, t : t + 1])
+            yv_planes.append(plane)
 
+        w3_rounded = [round_pair("w3_rounded%d" % pair, w3_raw, pair, "vector") for pair in range(2)]
+        w3_mx = [quantise("w3_mx%d" % pair, w3_rounded[pair]) for pair in range(2)]
+        w1_rounded = [round_pair("w1_rounded%d" % pair, w1_raw, pair, ("scalar", "gpsimd")[pair]) for pair in range(2)]
 
-        def sector(h):
-            planes = []
+        sector = sbuf("sector", [P, 2, PACK, HALF], F32, after="w1_raw")
+
+        def fetch_sector(h):
             for t in range(PACK):
-                g = sector_values[:, PACK * h + t, :]
-                nc.scalar.activation(g, yv[t][:].indirect(sec_t[:, 16 * h : 16 * (h + 1)]), ACT.Copy, scale=0.5)
-                planes.append(g)
-            return planes
+                looked_up = yv_planes[t][:].indirect(entries(sec_list, HALF * h, HALF * (h + 1)))
+                nc.scalar.activation(sector[:, h, t, :], looked_up, ACT.Copy, scale=0.5)
 
-        w3_b = [round_pair("w3_b%d" % h, w3_raw, h, ["vector","vector"][h]) for h in range(2)]
-        w3_q = [quantise("w3_q%d" % h, w3_b[h][:]) for h in range(2)]
-        w1_b = [round_pair("w1_b%d" % h, w1_raw, h, ["scalar","gpsimd"][h]) for h in range(2)]
-        sector_values = keep.tile([P, 2 * PACK, HALF], F32, name="sector_values", tag="w1_raw", align_bytes=64)
-        vs = [sector(0)]
-        hid2_b = sb("hid2_b", [P, N * PACK], BF16)
+        fetch_sector(0)
+
+        hid2_woven = sbuf("hid2_woven", [P, N * PACK], BF16)
         ye_acc = []
-        for b in range(4):
+        for b in range(N // P):
             acc = bank("ye_acc%d" % b)
             for t in range(PACK):
-                product(acc[:, block(t)], w3_q[t // 2], block(t % 2), e_picked, block(b))
+                product(acc[:, block(t)], w3_mx[t // 2], block(t % 2), e_picked, block(b))
             ye_acc.append(acc)
-        for b in range(4):
+        for b in range(N // P):
             nc.vector.tensor_tensor(
-                hid2_b[:, N * b : N * (b + 1)].rearrange("p (c i t) -> p c t i", i=2, t=PACK),
+                hid2_woven[:, N * b : N * (b + 1)].rearrange("p (c i t) -> p c t i", i=2, t=PACK),
                 ye_acc[b][:].rearrange("p (t c i) -> p c t i", i=2, t=PACK),
-                unit2_t[:].unsqueeze(1).unsqueeze(3).to_broadcast([P, P // 2, PACK, 2]),
+                unit2_rows[:].unsqueeze(1).unsqueeze(3).to_broadcast([P, P // 2, PACK, 2]),
                 ALU.mult,
             )
-        w1_q = [quantise("w1_q%d" % h, w1_b[h][:]) for h in range(2)]
-        hid2_q = quantise("hid2_q", hid2_b[:])
+        w1_mx = [quantise("w1_mx%d" % pair, w1_rounded[pair]) for pair in range(2)]
+        hid2_mx = quantise("hid2_mx", hid2_woven)
         y_acc = []
         for t in range(PACK):
             acc = bank("y_acc%d" % t)
-            product(acc[:], w1_q[t // 2], block(t % 2), x_picked, slice(0, N))
+            product(acc[:], w1_mx[t // 2], block(t % 2), x_picked, every)
             y_acc.append(acc)
-        vs.append(sector(1))
+        fetch_sector(1)
 
         def hid_planes(h):
-            planes = keep.tile([P, PACK, HALF], BF16, name="hid_planes%d" % h, tag="hid_planes", align_bytes=64)
+            planes = sbuf("hid_planes%d" % h, [P, PACK, HALF], BF16, after="hid_planes0")
             for t in range(PACK):
                 nc.vector.scalar_tensor_tensor(
-                    planes[:, t, :], y_acc[t][:, HALF * h : HALF * (h + 1)], unit_t[:, t : t + 1], vs[h][t], ALU.mult, ALU.add
+                    planes[:, t, :],
+                    y_acc[t][:, HALF * h : HALF * (h + 1)],
+                    unit_rows[:, t : t + 1],
+                    sector[:, h, t, :],
+                    ALU.mult,
+                    ALU.add,
                 )
             return planes
 
-        def weave(h, planes, on_scalar):
-            woven = keep.tile([P, PACK * HALF], BF16, name="hid_b%d" % h, tag="hid_b%d" % h, align_bytes=64)
-            dst = woven[:].rearrange("p (c i t) -> p c t i", i=4, t=PACK)
-            src = planes[:].rearrange("p t (c i) -> p c t i", i=4)
-            if on_scalar:
-                nc.scalar.copy(dst, src)
-            else:
-                nc.vector.tensor_copy(dst, src)
+        def weave(h, planes):
+            woven = sbuf("hid_woven%d" % h, [P, PACK * HALF], BF16)
+            nc.vector.tensor_copy(
+                woven[:].rearrange("p (c i t) -> p c t i", i=4, t=PACK), planes[:].rearrange("p t (c i) -> p c t i", i=4)
+            )
             return woven
 
-        def covariances(b, hid_q):
+        def covariances(b, hid_mx):
             acc = bank("sc_acc%d" % b)
-            product(acc[:], hid_q, block(b % 2), hid2_q, slice(0, N))
+            product(acc[:], hid_mx, block(b % 2), hid2_mx, every)
             return acc
 
-        def betas(b, acc, total):
-            nc.vector.tensor_tensor(beta[b][:, :N], acc[:], inv_vol[:], ALU.mult)
+        def betas(b, acc, totals):
+            nc.vector.tensor_tensor(scaled_beta[b][:, :N], acc[:], inv_vol[:], ALU.mult)
             squares = keep.tile([P, N], BF16, name="squares%d" % b, tag="squares", bufs=2)
-            nc.scalar.activation(squares[:], beta[b][:, :N], ACT.Square, accum_out=total)
+            nc.scalar.activation(squares[:], scaled_beta[b][:, :N], ACT.Square, accum_out=totals[:, b % 2 : b % 2 + 1])
 
-        def roots(h, totals):
-            root = sb("root%d" % h, [P, 2], F32)
-            nc.scalar.activation(root[:], totals[:], ACT.Sqrt, scale=1.0 / (0.16 * N), bias=0.1)
-            return root
+        def square_roots(h, totals):
+            roots = sbuf("roots%d" % h, [P, 2], F32)
+            nc.scalar.activation(roots[:], totals[:], ACT.Sqrt, scale=1.0 / (0.16 * N), bias=0.1)
+            return roots
 
-        def factors(h, root, denom):
-            nc.vector.tensor_scalar(denom[:], root[:], 0.4, 0.12, ALU.mult, ALU.add)
-            factor = sb("factor%d" % h, [P, 2], F32)
-            nc.vector.reciprocal(factor[:], denom[:])
-            return factor
+        def row_factors(h, roots, after=None):
+            denoms = sbuf("denoms%d" % h, [P, 2], F32, after=after)
+            nc.vector.tensor_scalar(denoms[:], roots[:], 0.4, 0.12, ALU.mult, ALU.add)
+            factors = sbuf("factors%d" % h, [P, 2], F32)
+            nc.vector.reciprocal(factors[:], denoms[:])
+            return factors
 
-        def looked_up(b, lo, hi):
-            return beta[b][:].indirect(prx_t[:, lo // 16 : hi // 16])
+        def proxy_operand(b, lo, hi):
+            return scaled_beta[b][:].indirect(entries(prx_list, lo, hi))
 
-        def finish(b, lo, hi, factor, proxy):
-            result = sb("result%d_%d" % (b, lo), [P, hi - lo], F32)
+        def finish(b, lo, hi, factors, proxy):
+            result = sbuf("result%d_%d" % (b, lo), [P, hi - lo], F32)
             nc.vector.scalar_tensor_tensor(
-                result[:], beta[b][:, lo:hi], factor[:, b % 2 : b % 2 + 1], proxy, ALU.mult, ALU.subtract
+                result[:], scaled_beta[b][:, lo:hi], factors[:, b % 2 : b % 2 + 1], proxy, ALU.mult, ALU.subtract
             )
             nc.sync.dma_start(out[block(b), lo:hi], result[:])
 
-        def shared(name, tag, shape, dtype):
-            return keep.tile(shape, dtype, name=name, tag=tag, align_bytes=64)
-
-        planes0 = hid_planes(0)
-        woven0 = weave(0, planes0, False)
-        hid_q0 = quantise("hid_q0", woven0[:])
-        acc0 = covariances(0, hid_q0)
-        acc1 = covariances(1, hid_q0)
-        totals0 = shared("totals0", "proxies0", [P, 2], F32)
-        betas(0, acc0, totals0[:, 0:1])
-        betas(1, acc1, totals0[:, 1:2])
-        root0 = roots(0, totals0)
-        proxies0 = shared("proxies0", "proxies0", [P, 2, N], F32)
-        for b in range(2):
-            nc.scalar.activation(proxies0[:, b, :], looked_up(b, 0, N), ACT.Copy)
+        hid_mx0 = quantise("hid_mx0", weave(0, hid_planes(0)))
+        sc_acc0 = covariances(0, hid_mx0)
+        sc_acc1 = covariances(1, hid_mx0)
         planes1 = hid_planes(1)
-        woven1 = weave(1, planes1, False)
-        hid_q1 = quantise("hid_q1", woven1[:])
-        factor0 = factors(0, root0, shared("denom0", "hid_b1", [P, 2], F32))
-        acc2 = covariances(2, hid_q1)
-        acc3 = covariances(3, hid_q1)
-        totals1 = shared("totals1", "proxies1", [P, 2], F32)
-        betas(2, acc2, totals1[:, 0:1])
-        betas(3, acc3, totals1[:, 1:2])
-        root1 = roots(1, totals1)
-        finish(0, 0, N, factor0, proxies0[:, 0, :])
-        proxy_first = sb("proxy_first", [P, HALF], F32)
-        nc.vector.tensor_copy(proxy_first[:], looked_up(2, 0, HALF))
-        proxies1 = shared("proxies1", "proxies1", [P, 3, HALF], F32)
-        pieces = [(2, HALF), (3, 0), (3, HALF)]
-        for i, (b, lo) in enumerate(pieces):
-            nc.scalar.activation(proxies1[:, i, :], looked_up(b, lo, lo + HALF), ACT.Copy)
-        finish(1, 0, N, factor0, proxies0[:, 1, :])
-        factor1 = factors(1, root1, sb("denom1", [P, 2], F32))
-        finish(2, 0, HALF, factor1, proxy_first[:])
-        for i, (b, lo) in enumerate(pieces):
-            finish(b, lo, lo + HALF, factor1, proxies1[:, i, :])
+        totals0 = sbuf("totals0", [P, 2], F32)
+        betas(0, sc_acc0, totals0)
+        proxy0 = sbuf("proxy0", [P, N], F32)
+        nc.scalar.activation(proxy0[:], proxy_operand(0, 0, N), ACT.Copy)
+        woven1 = weave(1, planes1)
+        betas(1, sc_acc1, totals0)
+        roots0 = square_roots(0, totals0)
+        proxy1 = sbuf("proxy1", [P, N], F32, after="totals0")
+        nc.scalar.activation(proxy1[:], proxy_operand(1, 0, N), ACT.Copy)
+        hid_mx1 = quantise("hid_mx1", woven1)
+        factors0 = row_factors(0, roots0, after="hid_woven1")
+        sc_acc2 = covariances(2, hid_mx1)
+        sc_acc3 = covariances(3, hid_mx1)
+        totals1 = sbuf("totals1", [P, 2], F32)
+        betas(2, sc_acc2, totals1)
+        betas(3, sc_acc3, totals1)
+        roots1 = square_roots(1, totals1)
+        finish(0, 0, N, factors0, proxy0[:])
+        proxy2_head = sbuf("proxy2_head", [P, CUT], F32)
+        nc.vector.tensor_copy(proxy2_head[:], proxy_operand(2, 0, CUT))
+        last_proxies = sbuf("last_proxies", [P, 2 * N - CUT], F32, after="totals1")
+        pieces = [(2, CUT, N), (3, 0, CUT), (3, CUT, N)]
+
+        def place(b, lo, hi):
+            start = N * (b - 2) - CUT
+            return last_proxies[:, start + lo : start + hi]
+
+        for b, lo, hi in pieces:
+            nc.scalar.activation(place(b, lo, hi), proxy_operand(b, lo, hi), ACT.Copy)
+        finish(1, 0, N, factors0, proxy1[:])
+        factors1 = row_factors(1, roots1)
+        finish(2, 0, CUT, factors1, proxy2_head[:])
+        for b, lo, hi in pieces:
+            finish(b, lo, hi, factors1, place(b, lo, hi))

from contextlib import ExitStack

import concourse.mybir as mybir
from concourse.masks import make_identity

F32 = mybir.dt.float32
BF16 = mybir.dt.bfloat16
I32 = mybir.dt.int32
U32 = mybir.dt.uint32
U16 = mybir.dt.uint16
U8 = mybir.dt.uint8
FP8X4 = mybir.dt.float8_e4m3fn_x4
ALU = mybir.AluOpType
ACT = mybir.ActivationFunctionType

P = 128
PACK = 4
N = 512
STORE = 1024
HALF = N // 2
ENTRIES = 16
SPARE = 8
CUT = 384
BANKS = 8
FLOPS = 4 * 2 * N * N * N


def tile_picked_yfcovr_beta_p_kernel(
    tc, x_words, x_scales, w1, w2, e_words, e_scales, w3, unit, unit2, vol, offs, hdg, sec, prx, out
):
    nc = tc.nc
    with ExitStack() as ctx:
        keep = ctx.enter_context(tc.tile_pool(name="keep", bufs=1))
        psum = ctx.enter_context(tc.psum_pool(name="psum", bufs=BANKS))

        def sbuf(name, shape, dtype, after=None):
            return keep.tile(shape, dtype, name=name, tag=after or name, align_bytes=64)

        def bank(name):
            return psum.tile([P, N], F32, name=name, tag="bank")

        def block(b):
            return slice(P * b, P * (b + 1))

        def entries(list_tile, lo, hi):
            return list_tile[:, lo // ENTRIES : hi // ENTRIES]

        def load_list(name, src):
            tile = keep.tile([P, N // ENTRIES], U16, name=name)
            nc.sync.dma_start(tile[:], src)
            return tile

        def load_words(name, src):
            tile = sbuf(name, [P, STORE], U32)
            nc.sync.dma_start(tile[:].bitcast(I32), src[0].rearrange("p n r -> p (n r)").bitcast(I32))
            return tile

        def load_scales(name, src):
            tile = sbuf(name, [P, STORE], U8)
            nc.gpsimd.memset(tile[:].bitcast(I32), 0)
            for q in range(4):
                nc.sync.dma_start(tile[32 * q : 32 * q + 4, :].bitcast(I32), src[0, 4 * q : 4 * q + 4, :].bitcast(I32))
            return tile

        def load_weight(name, src):
            tile = sbuf(name, [P, PACK, N], F32)
            nc.sync.dma_start(tile[:], src.rearrange("(p j) c -> p j c", j=PACK))
            return tile

        def load_row_factors(name, src):
            tile = sbuf(name, [P, PACK], F32)
            nc.gpsimd.dma_start(tile[:], src.rearrange("(p t) o -> p (t o)", t=PACK))
            return tile

        def pick(name, table, list_tile, dtype):
            tile = sbuf(name, [P, N], dtype)
            nc.vector.tensor_copy(tile[:], table[:].indirect(list_tile[:]))
            return tile

        def round_pair(name, raw, pair, engine):
            tile = sbuf(name, [P, 2 * N], BF16)
            dst = tile[:].rearrange("p (t m j) -> p m j t", t=2, j=PACK)
            src = raw[:].rearrange("p j (m t) -> p m j t", t=PACK)[:, :, :, 2 * pair : 2 * pair + 2]
            if engine == "scalar":
                nc.scalar.copy(dst, src)
            elif engine == "vector":
                nc.vector.tensor_copy(dst, src)
            else:
                nc.gpsimd.tensor_scalar(
                    dst.rearrange("p m j t -> p m t j"), src.rearrange("p m j t -> p m t j"), 1.0, 0.0, ALU.mult, ALU.add
                )
            return tile

        def quantise(name, values):
            width = values.shape[1] // PACK
            codes = sbuf(name + "_codes", [P, width], U32)
            scales = sbuf(name + "_scales", [P, width], U8)
            nc.vector.quantize_mx(codes[:].bitcast(FP8X4), scales[:], values[:])
            return codes, scales

        def product(dst, lhs, lhs_cols, rhs, rhs_cols):
            nc.tensor.matmul_mx(
                dst,
                lhsT=lhs[0][:, lhs_cols].bitcast(FP8X4),
                lhsT_scale=lhs[1][:, lhs_cols],
                rhs=rhs[0][:, rhs_cols].bitcast(FP8X4),
                rhs_scale=rhs[1][:, rhs_cols],
                start=True,
                stop=True,
            )

        every = slice(0, N)

        offs_list = load_list("offs_list", offs)
        vol_narrow = sbuf("vol_narrow", [P, STORE // P], F32)
        nc.sync.dma_start(vol_narrow[:], vol[0, :].rearrange("(n m) -> n m", n=P))
        x_scale_table = load_scales("x_scale_table", x_scales)
        x_word_table = load_words("x_word_table", x_words)
        e_word_table = load_words("e_word_table", e_words)
        hdg_list = load_list("hdg_list", hdg)
        e_scale_table = load_scales("e_scale_table", e_scales)
        w2_raw = load_weight("w2_raw", w2)
        w3_raw = load_weight("w3_raw", w3)
        sec_list = load_list("sec_list", sec)
        w1_raw = load_weight("w1_raw", w1)
        prx_list = load_list("prx_list", prx)
        identity = sbuf("identity", [P, P], F32)
        make_identity(nc, identity[:])
        unit_rows = load_row_factors("unit_rows", unit)
        unit2_rows = load_row_factors("unit2_rows", unit2)

        warm_in = sbuf("warm_in", [P, 1], F32)
        nc.vector.memset(warm_in[:], 1.0)
        warm_out = sbuf("warm_out", [P, 1], F32)
        nc.scalar.activation(warm_out[:], warm_in[:], ACT.Sqrt)

        scaled_beta = [sbuf("scaled_beta%d" % b, [P, N + SPARE], F32) for b in range(N // P)]
        for b in range(N // P):
            nc.gpsimd.memset(scaled_beta[b][:, N:], 0.0)

        inv_narrow = sbuf("inv_narrow", [P, STORE // P], F32)
        nc.vector.reciprocal(inv_narrow[:], vol_narrow[:])
        x_picked_scales = pick("x_picked_scales", x_scale_table, offs_list, U8)
        x_picked = (pick("x_picked_words", x_word_table, offs_list, U32), x_picked_scales)
        inv_table = sbuf("inv_table", [P, STORE], F32)
        for h in range(2):
            spread = bank("spread%d" % h)
            for m in range(4):
                column = inv_narrow[:, 4 * h + m : 4 * h + m + 1]
                nc.tensor.transpose(spread[:, block(m)], column.to_broadcast([P, P]), identity[:])
            nc.scalar.activation(
                inv_table[:].rearrange("p (n h m) -> p h n m", h=2, m=4)[:, h],
                spread[:].rearrange("p (m n) -> p n m", m=4),
                ACT.Copy,
                scale=0.4,
            )
        inv_vol = sbuf("inv_vol", [P, N], F32)
        nc.scalar.activation(inv_vol[:], inv_table[:].indirect(hdg_list[:]), ACT.Copy)

        e_picked_words = pick("e_picked_words", e_word_table, hdg_list, U32)
        e_picked = (e_picked_words, pick("e_picked_scales", e_scale_table, hdg_list, U8))

        w2_rounded = [round_pair("w2_rounded%d" % pair, w2_raw, pair, ("vector", "scalar")[pair]) for pair in range(2)]
        w2_mx = [quantise("w2_mx%d" % pair, w2_rounded[pair]) for pair in range(2)]
        yv_planes = []
        for t in range(PACK):
            acc = bank("yv_acc%d" % t)
            product(acc[:], w2_mx[t // 2], block(t % 2), x_picked, every)
            plane = sbuf("yv_plane%d" % t, [P, N], F32)
            nc.scalar.activation(plane[:], acc[:], ACT.Copy, scale=unit_rows[:, t : t + 1])
            yv_planes.append(plane)

        w3_rounded = [round_pair("w3_rounded%d" % pair, w3_raw, pair, "vector") for pair in range(2)]
        w3_mx = [quantise("w3_mx%d" % pair, w3_rounded[pair]) for pair in range(2)]
        w1_rounded = [round_pair("w1_rounded%d" % pair, w1_raw, pair, ("scalar", "gpsimd")[pair]) for pair in range(2)]

        sector = sbuf("sector", [P, 2, PACK, HALF], F32, after="w1_raw")

        def fetch_sector(h):
            for t in range(PACK):
                looked_up = yv_planes[t][:].indirect(entries(sec_list, HALF * h, HALF * (h + 1)))
                nc.scalar.activation(sector[:, h, t, :], looked_up, ACT.Copy, scale=0.5)

        fetch_sector(0)

        hid2_woven = sbuf("hid2_woven", [P, N * PACK], BF16)
        ye_acc = []
        for b in range(N // P):
            acc = bank("ye_acc%d" % b)
            for t in range(PACK):
                product(acc[:, block(t)], w3_mx[t // 2], block(t % 2), e_picked, block(b))
            ye_acc.append(acc)
        for b in range(N // P):
            nc.vector.tensor_tensor(
                hid2_woven[:, N * b : N * (b + 1)].rearrange("p (c i t) -> p c t i", i=2, t=PACK),
                ye_acc[b][:].rearrange("p (t c i) -> p c t i", i=2, t=PACK),
                unit2_rows[:].unsqueeze(1).unsqueeze(3).to_broadcast([P, P // 2, PACK, 2]),
                ALU.mult,
            )
        w1_mx = [quantise("w1_mx%d" % pair, w1_rounded[pair]) for pair in range(2)]
        hid2_mx = quantise("hid2_mx", hid2_woven)
        y_acc = []
        for t in range(PACK):
            acc = bank("y_acc%d" % t)
            product(acc[:], w1_mx[t // 2], block(t % 2), x_picked, every)
            y_acc.append(acc)
        fetch_sector(1)

        def hid_planes(h):
            planes = sbuf("hid_planes%d" % h, [P, PACK, HALF], BF16, after="hid_planes0")
            for t in range(PACK):
                nc.vector.scalar_tensor_tensor(
                    planes[:, t, :],
                    y_acc[t][:, HALF * h : HALF * (h + 1)],
                    unit_rows[:, t : t + 1],
                    sector[:, h, t, :],
                    ALU.mult,
                    ALU.add,
                )
            return planes

        def weave(h, planes):
            woven = sbuf("hid_woven%d" % h, [P, PACK * HALF], BF16)
            nc.vector.tensor_copy(
                woven[:].rearrange("p (c i t) -> p c t i", i=4, t=PACK), planes[:].rearrange("p t (c i) -> p c t i", i=4)
            )
            return woven

        def covariances(b, hid_mx):
            acc = bank("sc_acc%d" % b)
            product(acc[:], hid_mx, block(b % 2), hid2_mx, every)
            return acc

        def betas(b, acc, totals):
            nc.vector.tensor_tensor(scaled_beta[b][:, :N], acc[:], inv_vol[:], ALU.mult)
            squares = keep.tile([P, N], BF16, name="squares%d" % b, tag="squares", bufs=2)
            nc.scalar.activation(squares[:], scaled_beta[b][:, :N], ACT.Square, accum_out=totals[:, b % 2 : b % 2 + 1])

        def square_roots(h, totals):
            roots = sbuf("roots%d" % h, [P, 2], F32)
            nc.scalar.activation(roots[:], totals[:], ACT.Sqrt, scale=1.0 / (0.16 * N), bias=0.1)
            return roots

        def row_factors(h, roots, after=None):
            denoms = sbuf("denoms%d" % h, [P, 2], F32, after=after)
            nc.vector.tensor_scalar(denoms[:], roots[:], 0.4, 0.12, ALU.mult, ALU.add)
            factors = sbuf("factors%d" % h, [P, 2], F32)
            nc.vector.reciprocal(factors[:], denoms[:])
            return factors

        def proxy_operand(b, lo, hi):
            return scaled_beta[b][:].indirect(entries(prx_list, lo, hi))

        def finish(b, lo, hi, factors, proxy):
            result = sbuf("result%d_%d" % (b, lo), [P, hi - lo], F32)
            nc.vector.scalar_tensor_tensor(
                result[:], scaled_beta[b][:, lo:hi], factors[:, b % 2 : b % 2 + 1], proxy, ALU.mult, ALU.subtract
            )
            nc.sync.dma_start(out[block(b), lo:hi], result[:])

        hid_mx0 = quantise("hid_mx0", weave(0, hid_planes(0)))
        sc_acc0 = covariances(0, hid_mx0)
        sc_acc1 = covariances(1, hid_mx0)
        planes1 = hid_planes(1)
        totals0 = sbuf("totals0", [P, 2], F32)
        betas(0, sc_acc0, totals0)
        proxy0 = sbuf("proxy0", [P, N], F32)
        nc.scalar.activation(proxy0[:], proxy_operand(0, 0, N), ACT.Copy)
        woven1 = weave(1, planes1)
        betas(1, sc_acc1, totals0)
        roots0 = square_roots(0, totals0)
        proxy1 = sbuf("proxy1", [P, N], F32, after="totals0")
        nc.scalar.activation(proxy1[:], proxy_operand(1, 0, N), ACT.Copy)
        hid_mx1 = quantise("hid_mx1", woven1)
        factors0 = row_factors(0, roots0, after="hid_woven1")
        sc_acc2 = covariances(2, hid_mx1)
        sc_acc3 = covariances(3, hid_mx1)
        totals1 = sbuf("totals1", [P, 2], F32)
        betas(2, sc_acc2, totals1)
        betas(3, sc_acc3, totals1)
        roots1 = square_roots(1, totals1)
        finish(0, 0, N, factors0, proxy0[:])
        proxy2_head = sbuf("proxy2_head", [P, CUT], F32)
        nc.vector.tensor_copy(proxy2_head[:], proxy_operand(2, 0, CUT))
        last_proxies = sbuf("last_proxies", [P, 2 * N - CUT], F32, after="totals1")
        pieces = [(2, CUT, N), (3, 0, CUT), (3, CUT, N)]

        def place(b, lo, hi):
            start = N * (b - 2) - CUT
            return last_proxies[:, start + lo : start + hi]

        for b, lo, hi in pieces:
            nc.scalar.activation(place(b, lo, hi), proxy_operand(b, lo, hi), ACT.Copy)
        finish(1, 0, N, factors0, proxy1[:])
        factors1 = row_factors(1, roots1)
        finish(2, 0, CUT, factors1, proxy2_head[:])
        for b, lo, hi in pieces:
            finish(b, lo, hi, factors1, place(b, lo, hi))
